import numpy as np
import ml_dtypes

BF16 = ml_dtypes.bfloat16


def bf(x):
    return np.asarray(x, np.float32).astype(BF16)


def f32(x):
    return np.asarray(x, np.float32)


def f64(x):
    return np.asarray(x).astype(np.float64)


def striped(idx):
    return np.tile(idx.reshape(-1, 16).T, (8, 1))


S, K, M, N, E, Q = 512, 128, 128, 1024, 8, 128


def two_experts():
    first = np.random.permutation(S).reshape(E, S // E)
    return np.concatenate([np.random.permutation(np.concatenate([first[e], first[(e + 1) % E]])) for e in range(E)])


def setup_inputs():
    return {"table": bf(np.random.standard_normal((K, S))), "w": bf(np.random.standard_normal((E, K, M)) / np.sqrt(K)), "c": f32(0.2 + 0.8 * np.random.random_sample((1, N))), "offs": striped(two_experts())}


def reference(table, w, c, offs):
    idx = offs[:16].T.reshape(-1)
    x = f64(table)[:, idx]
    y = np.concatenate([f64(w)[e].T @ x[:, e * Q : (e + 1) * Q] for e in range(E)], axis=1)
    return y * f64(c)

@@ -1,0 +1,47 @@
+import concourse.mybir as mybir
+
+BF16, F32, U16 = mybir.dt.bfloat16, mybir.dt.float32, mybir.dt.uint16
+
+P = 128
+TOKENS = 512
+EXPERTS = 8
+PIECE = 128
+ENTRIES = EXPERTS * PIECE
+PIECE_COLS = PIECE // 16
+BANK = 512
+EXPERTS_IN_BANK = BANK // PIECE
+
+FLOPS = 2 * P * P * ENTRIES
+
+
+def tile_gather_matmul_kernel(tc, table, w, c, offs, out):
+    nc = tc.nc
+    with (
+        tc.tile_pool(name="held", bufs=1) as held,
+        tc.psum_pool(name="psum", bufs=1) as psum,
+    ):
+        offsets = held.tile([P, ENTRIES // 16], U16, name="offsets")
+        nc.sync.dma_start(offsets[:], offs)
+
+        tokens = held.tile([P, TOKENS], BF16, name="tokens")
+        nc.scalar.dma_start(tokens[:], table)
+
+        weights = held.tile([P, EXPERTS, P], BF16, name="weights")
+        nc.sync.dma_start(weights[:], w.rearrange("e k m -> k e m"))
+
+        gains = held.tile([P, ENTRIES], F32, name="gains")
+        nc.gpsimd.dma_start(gains[:], c.rearrange("o n -> (o n)").partition_broadcast(P))
+
+        scaled = held.tile([P, ENTRIES], F32, name="scaled")
+
+        for b in range(ENTRIES // BANK):
+            bank = psum.tile([P, BANK], F32, name=f"bank{b}")
+            for i in range(EXPERTS_IN_BANK):
+                e = b * EXPERTS_IN_BANK + i
+                picked = tokens[:].indirect(offsets[:, e * PIECE_COLS : (e + 1) * PIECE_COLS])
+                nc.tensor.matmul(
+                    bank[:, i * PIECE : (i + 1) * PIECE], weights[:, e, :], picked, start=True, stop=True
+                )
+            cols = slice(b * BANK, (b + 1) * BANK)
+            nc.vector.tensor_tensor(scaled[:, cols], bank[:], gains[:, cols], mybir.AluOpType.mult)
+            nc.sync.dma_start(out[:, cols], scaled[:, cols])

@@ -1,4 +1,5 @@
 import concourse.mybir as mybir
+from concourse.masks import make_identity
 
 BF16, F32, U16 = mybir.dt.bfloat16, mybir.dt.float32, mybir.dt.uint16
 
@@ -23,14 +24,29 @@ def tile_gather_matmul_kernel(tc, table, w, c, offs, out):
         offsets = held.tile([P, ENTRIES // 16], U16, name="offsets")
         nc.sync.dma_start(offsets[:], offs)
 
+        gain_columns = held.tile([P, EXPERTS], F32, name="gain_columns")
+        nc.scalar.dma_start(gain_columns[:], c.rearrange("o (e q) -> q (o e)", q=PIECE))
+
         tokens = held.tile([P, TOKENS], BF16, name="tokens")
         nc.scalar.dma_start(tokens[:], table)
 
         weights = held.tile([P, EXPERTS, P], BF16, name="weights")
         nc.sync.dma_start(weights[:], w.rearrange("e k m -> k e m"))
 
+        identity = held.tile([P, P], F32, name="identity")
+        make_identity(nc, identity[:])
+
         gains = held.tile([P, ENTRIES], F32, name="gains")
-        nc.gpsimd.dma_start(gains[:], c.rearrange("o n -> (o n)").partition_broadcast(P))
+        for b in range(ENTRIES // BANK):
+            spread = psum.tile([P, BANK], F32, name=f"spread{b}")
+            for i in range(EXPERTS_IN_BANK):
+                e = b * EXPERTS_IN_BANK + i
+                nc.tensor.transpose(
+                    spread[:, i * PIECE : (i + 1) * PIECE],
+                    gain_columns[:, e : e + 1].to_broadcast([P, P]),
+                    identity[:],
+                )
+            nc.vector.tensor_copy(gains[:, b * BANK : (b + 1) * BANK], spread[:])
 
         scaled = held.tile([P, ENTRIES], F32, name="scaled")
 

@@ -9,8 +9,12 @@ EXPERTS = 8
 PIECE = 128
 ENTRIES = EXPERTS * PIECE
 PIECE_COLS = PIECE // 16
+SHARE = 2
+SHARES = EXPERTS // SHARE
+WIDTH = SHARE * PIECE
+BLOCK = 8
 BANK = 512
-EXPERTS_IN_BANK = BANK // PIECE
+WARMUPS = 5
 
 FLOPS = 2 * P * P * ENTRIES
 
@@ -21,43 +25,60 @@ def tile_gather_matmul_kernel(tc, table, w, c, offs, out):
         tc.tile_pool(name="held", bufs=1) as held,
         tc.psum_pool(name="psum", bufs=1) as psum,
     ):
+        gain_columns = held.tile([P, SHARES, BLOCK], F32, name="gain_columns")
+        nc.sync.dma_start(
+            gain_columns[:, :, 0:SHARE], c.rearrange("o (t p s) -> p (o t) s", t=SHARES, s=SHARE)
+        )
+
         offsets = held.tile([P, ENTRIES // 16], U16, name="offsets")
         nc.sync.dma_start(offsets[:], offs)
 
-        gain_columns = held.tile([P, EXPERTS], F32, name="gain_columns")
-        nc.scalar.dma_start(gain_columns[:], c.rearrange("o (e q) -> q (o e)", q=PIECE))
-
         tokens = held.tile([P, TOKENS], BF16, name="tokens")
-        nc.scalar.dma_start(tokens[:], table)
+        nc.sync.dma_start(tokens[:], table)
 
         weights = held.tile([P, EXPERTS, P], BF16, name="weights")
-        nc.sync.dma_start(weights[:], w.rearrange("e k m -> k e m"))
+        nc.scalar.dma_start(weights[:], w.rearrange("e k m -> k e m"))
+
+        zero = held.tile([P, 1], BF16, name="zero")
+        nc.vector.memset(zero[:], 0.0)
+        unread = psum.tile([P, BANK], F32, name="unread")
+        for n in range(WARMUPS):
+            nc.tensor.matmul(
+                unread[:], zero[:].to_broadcast([P, P]), zero[:].to_broadcast([P, BANK]), start=True, stop=True
+            )
+
+        primer = held.tile([P, 2], F32, name="primer")
+        nc.gpsimd.memset(primer[:, 0:1], 0.0)
+        nc.scalar.copy(primer[:, 1:2], primer[:, 0:1])
 
         identity = held.tile([P, P], F32, name="identity")
         make_identity(nc, identity[:])
 
         gains = held.tile([P, ENTRIES], F32, name="gains")
-        for b in range(ENTRIES // BANK):
-            spread = psum.tile([P, BANK], F32, name=f"spread{b}")
-            for i in range(EXPERTS_IN_BANK):
-                e = b * EXPERTS_IN_BANK + i
+        for t in range(SHARES):
+            spread = psum.tile([P, WIDTH], F32, name=f"spread{t}", tag=f"share{t}")
+            for s in range(SHARE):
                 nc.tensor.transpose(
-                    spread[:, i * PIECE : (i + 1) * PIECE],
-                    gain_columns[:, e : e + 1].to_broadcast([P, P]),
+                    spread[:, s * P : (s + 1) * P],
+                    gain_columns[:, t, s : s + 1].to_broadcast([P, P]),
                     identity[:],
                 )
-            nc.vector.tensor_copy(gains[:, b * BANK : (b + 1) * BANK], spread[:])
+            nc.scalar.copy(
+                gains[:, t * WIDTH : (t + 1) * WIDTH].rearrange("m (p s) -> m p s", s=SHARE),
+                spread[:].rearrange("m (s p) -> m p s", s=SHARE),
+            )
 
         scaled = held.tile([P, ENTRIES], F32, name="scaled")
 
-        for b in range(ENTRIES // BANK):
-            bank = psum.tile([P, BANK], F32, name=f"bank{b}")
-            for i in range(EXPERTS_IN_BANK):
-                e = b * EXPERTS_IN_BANK + i
+        for t in range(SHARES):
+            products = psum.tile([P, WIDTH], F32, name=f"products{t}", tag=f"share{t}")
+            for i in range(SHARE):
+                e = t * SHARE + i
                 picked = tokens[:].indirect(offsets[:, e * PIECE_COLS : (e + 1) * PIECE_COLS])
                 nc.tensor.matmul(
-                    bank[:, i * PIECE : (i + 1) * PIECE], weights[:, e, :], picked, start=True, stop=True
+                    products[:, i * PIECE : (i + 1) * PIECE], weights[:, e, :], picked, start=True, stop=True
                 )
-            cols = slice(b * BANK, (b + 1) * BANK)
-            nc.vector.tensor_tensor(scaled[:, cols], bank[:], gains[:, cols], mybir.AluOpType.mult)
-            nc.sync.dma_start(out[:, cols], scaled[:, cols])
+            cols = slice(t * WIDTH, (t + 1) * WIDTH)
+            nc.vector.tensor_tensor(scaled[:, cols], products[:], gains[:, cols], mybir.AluOpType.mult)
+            queue = nc.sync if t % 2 == 0 else nc.scalar
+            queue.dma_start(out[:, cols], scaled[:, cols])

@@ -13,8 +13,6 @@ SHARE = 2
 SHARES = EXPERTS // SHARE
 WIDTH = SHARE * PIECE
 BLOCK = 8
-BANK = 512
-WARMUPS = 5
 
 FLOPS = 2 * P * P * ENTRIES
 
@@ -38,14 +36,6 @@ def tile_gather_matmul_kernel(tc, table, w, c, offs, out):
 
         weights = held.tile([P, EXPERTS, P], BF16, name="weights")
         nc.scalar.dma_start(weights[:], w.rearrange("e k m -> k e m"))
-
-        zero = held.tile([P, 1], BF16, name="zero")
-        nc.vector.memset(zero[:], 0.0)
-        unread = psum.tile([P, BANK], F32, name="unread")
-        for n in range(WARMUPS):
-            nc.tensor.matmul(
-                unread[:], zero[:].to_broadcast([P, P]), zero[:].to_broadcast([P, BANK]), start=True, stop=True
-            )
 
         primer = held.tile([P, 2], F32, name="primer")
         nc.gpsimd.memset(primer[:, 0:1], 0.0)

@@ -34,8 +34,11 @@ def tile_gather_matmul_kernel(tc, table, w, c, offs, out):
         tokens = held.tile([P, TOKENS], BF16, name="tokens")
         nc.sync.dma_start(tokens[:], table)
 
-        weights = held.tile([P, EXPERTS, P], BF16, name="weights")
-        nc.scalar.dma_start(weights[:], w.rearrange("e k m -> k e m"))
+        weights = []
+        for t in range(SHARES):
+            matrices = held.tile([P, SHARE, P], BF16, name=f"weights{t}")
+            nc.scalar.dma_start(matrices[:], w[t * SHARE : (t + 1) * SHARE].rearrange("e k m -> k e m"))
+            weights.append(matrices)
 
         primer = held.tile([P, 2], F32, name="primer")
         nc.gpsimd.memset(primer[:, 0:1], 0.0)
@@ -66,7 +69,7 @@ def tile_gather_matmul_kernel(tc, table, w, c, offs, out):
                 e = t * SHARE + i
                 picked = tokens[:].indirect(offsets[:, e * PIECE_COLS : (e + 1) * PIECE_COLS])
                 nc.tensor.matmul(
-                    products[:, i * PIECE : (i + 1) * PIECE], weights[:, e, :], picked, start=True, stop=True
+                    products[:, i * PIECE : (i + 1) * PIECE], weights[t][:, i, :], picked, start=True, stop=True
                 )
             cols = slice(t * WIDTH, (t + 1) * WIDTH)
             nc.vector.tensor_tensor(scaled[:, cols], products[:], gains[:, cols], mybir.AluOpType.mult)

@@ -37,7 +37,7 @@ def tile_gather_matmul_kernel(tc, table, w, c, offs, out):
         weights = []
         for t in range(SHARES):
             matrices = held.tile([P, SHARE, P], BF16, name=f"weights{t}")
-            nc.scalar.dma_start(matrices[:], w[t * SHARE : (t + 1) * SHARE].rearrange("e k m -> k e m"))
+            nc.sync.dma_start(matrices[:], w[t * SHARE : (t + 1) * SHARE].rearrange("e k m -> k e m"))
             weights.append(matrices)
 
         primer = held.tile([P, 2], F32, name="primer")

@@ -13,6 +13,8 @@ SHARE = 2
 SHARES = EXPERTS // SHARE
 WIDTH = SHARE * PIECE
 BLOCK = 8
+BANK = 512
+WARMUPS = 4
 
 FLOPS = 2 * P * P * ENTRIES
 
@@ -39,6 +41,14 @@ def tile_gather_matmul_kernel(tc, table, w, c, offs, out):
             matrices = held.tile([P, SHARE, P], BF16, name=f"weights{t}")
             nc.sync.dma_start(matrices[:], w[t * SHARE : (t + 1) * SHARE].rearrange("e k m -> k e m"))
             weights.append(matrices)
+
+        zero = held.tile([P, 1], BF16, name="zero")
+        nc.vector.memset(zero[:], 0.0)
+        unread = psum.tile([P, BANK], F32, name="unread")
+        for n in range(WARMUPS):
+            nc.tensor.matmul(
+                unread[:], zero[:].to_broadcast([P, P]), zero[:].to_broadcast([P, BANK]), start=True, stop=True
+            )
 
         primer = held.tile([P, 2], F32, name="primer")
         nc.gpsimd.memset(primer[:, 0:1], 0.0)

@@ -73,15 +73,21 @@ def tile_gather_matmul_kernel(tc, table, w, c, offs, out):
 
         scaled = held.tile([P, ENTRIES], F32, name="scaled")
 
-        for t in range(SHARES):
-            products = psum.tile([P, WIDTH], F32, name=f"products{t}", tag=f"share{t}")
-            for i in range(SHARE):
-                e = t * SHARE + i
+        pieces = [(t * SHARE, SHARE) for t in range(SHARES - 1)]
+        pieces += [(e, 1) for e in range(EXPERTS - SHARE, EXPERTS)]
+        for n, (first, count) in enumerate(pieces):
+            products = psum.tile([P, count * PIECE], F32, name=f"products{n}", tag=f"share{n % SHARES}")
+            for i in range(count):
+                e = first + i
                 picked = tokens[:].indirect(offsets[:, e * PIECE_COLS : (e + 1) * PIECE_COLS])
                 nc.tensor.matmul(
-                    products[:, i * PIECE : (i + 1) * PIECE], weights[t][:, i, :], picked, start=True, stop=True
+                    products[:, i * PIECE : (i + 1) * PIECE],
+                    weights[e // SHARE][:, e % SHARE, :],
+                    picked,
+                    start=True,
+                    stop=True,
                 )
-            cols = slice(t * WIDTH, (t + 1) * WIDTH)
+            cols = slice(first * PIECE, (first + count) * PIECE)
             nc.vector.tensor_tensor(scaled[:, cols], products[:], gains[:, cols], mybir.AluOpType.mult)
-            queue = nc.sync if t % 2 == 0 else nc.scalar
+            queue = nc.sync if n % 2 == 0 else nc.scalar
             queue.dma_start(out[:, cols], scaled[:, cols])

@@ -66,10 +66,12 @@ def tile_gather_matmul_kernel(tc, table, w, c, offs, out):
                     gain_columns[:, t, s : s + 1].to_broadcast([P, P]),
                     identity[:],
                 )
-            nc.scalar.copy(
-                gains[:, t * WIDTH : (t + 1) * WIDTH].rearrange("m (p s) -> m p s", s=SHARE),
-                spread[:].rearrange("m (s p) -> m p s", s=SHARE),
-            )
+            in_order = gains[:, t * WIDTH : (t + 1) * WIDTH].rearrange("m (p s) -> m p s", s=SHARE)
+            as_spread = spread[:].rearrange("m (s p) -> m p s", s=SHARE)
+            if t % 2 == 0:
+                nc.scalar.copy(in_order, as_spread)
+            else:
+                nc.vector.tensor_copy(in_order, as_spread)
 
         scaled = held.tile([P, ENTRIES], F32, name="scaled")
 

@@ -75,7 +75,8 @@ def tile_gather_matmul_kernel(tc, table, w, c, offs, out):
 
         scaled = held.tile([P, ENTRIES], F32, name="scaled")
 
-        pieces = [(t * SHARE, SHARE) for t in range(SHARES - 1)]
+        pieces = [(e, 1) for e in range(SHARE)]
+        pieces += [(t * SHARE, SHARE) for t in range(1, SHARES - 1)]
         pieces += [(e, 1) for e in range(EXPERTS - SHARE, EXPERTS)]
         for n, (first, count) in enumerate(pieces):
             products = psum.tile([P, count * PIECE], F32, name=f"products{n}", tag=f"share{n % SHARES}")

@@ -42,20 +42,24 @@ def tile_gather_matmul_kernel(tc, table, w, c, offs, out):
             nc.sync.dma_start(matrices[:], w[t * SHARE : (t + 1) * SHARE].rearrange("e k m -> k e m"))
             weights.append(matrices)
 
-        zero = held.tile([P, 1], BF16, name="zero")
-        nc.vector.memset(zero[:], 0.0)
-        unread = psum.tile([P, BANK], F32, name="unread")
-        for n in range(WARMUPS):
-            nc.tensor.matmul(
-                unread[:], zero[:].to_broadcast([P, P]), zero[:].to_broadcast([P, BANK]), start=True, stop=True
-            )
-
         primer = held.tile([P, 2], F32, name="primer")
         nc.gpsimd.memset(primer[:, 0:1], 0.0)
         nc.scalar.copy(primer[:, 1:2], primer[:, 0:1])
 
         identity = held.tile([P, P], F32, name="identity")
         make_identity(nc, identity[:])
+
+        zero = held.tile([P, 1], BF16, name="zero")
+        nc.vector.memset(zero[:], 0.0)
+        unread = psum.tile([P, BANK], F32, name="unread")
+        nc.tensor.matmul(
+            unread[:], zero[:].to_broadcast([P, P]), zero[:].to_broadcast([P, BANK]), start=True, stop=True
+        )
+        for n in range(WARMUPS - 1):
+            warm = psum.tile([P, BANK], F32, name=f"warm{n}", tag=f"own{n}")
+            nc.tensor.matmul(
+                warm[:], identity[:].bitcast(BF16)[:, 0:P], zero[:].to_broadcast([P, BANK]), start=True, stop=True
+            )
 
         gains = held.tile([P, ENTRIES], F32, name="gains")
         for t in range(SHARES):
@@ -78,8 +82,9 @@ def tile_gather_matmul_kernel(tc, table, w, c, offs, out):
         pieces = [(e, 1) for e in range(SHARE)]
         pieces += [(t * SHARE, SHARE) for t in range(1, SHARES - 1)]
         pieces += [(e, 1) for e in range(EXPERTS - SHARE, EXPERTS)]
+        slots = [f"own{n}" for n in range(WARMUPS - 1)] + [f"share{t}" for t in range(SHARES)]
         for n, (first, count) in enumerate(pieces):
-            products = psum.tile([P, count * PIECE], F32, name=f"products{n}", tag=f"share{n % SHARES}")
+            products = psum.tile([P, count * PIECE], F32, name=f"products{n}", tag=slots[n])
             for i in range(count):
                 e = first + i
                 picked = tokens[:].indirect(offsets[:, e * PIECE_COLS : (e + 1) * PIECE_COLS])

@@ -72,10 +72,7 @@ def tile_gather_matmul_kernel(tc, table, w, c, offs, out):
                 )
             in_order = gains[:, t * WIDTH : (t + 1) * WIDTH].rearrange("m (p s) -> m p s", s=SHARE)
             as_spread = spread[:].rearrange("m (s p) -> m p s", s=SHARE)
-            if t % 2 == 0:
-                nc.scalar.copy(in_order, as_spread)
-            else:
-                nc.vector.tensor_copy(in_order, as_spread)
+            nc.scalar.copy(in_order, as_spread)
 
         scaled = held.tile([P, ENTRIES], F32, name="scaled")
 

@@ -72,7 +72,10 @@ def tile_gather_matmul_kernel(tc, table, w, c, offs, out):
                 )
             in_order = gains[:, t * WIDTH : (t + 1) * WIDTH].rearrange("m (p s) -> m p s", s=SHARE)
             as_spread = spread[:].rearrange("m (s p) -> m p s", s=SHARE)
-            nc.scalar.copy(in_order, as_spread)
+            if t < SHARES // 2:
+                nc.vector.tensor_copy(in_order, as_spread)
+            else:
+                nc.scalar.copy(in_order, as_spread)
 
         scaled = held.tile([P, ENTRIES], F32, name="scaled")
 

import concourse.mybir as mybir
from concourse.masks import make_identity

BF16, F32, U16 = mybir.dt.bfloat16, mybir.dt.float32, mybir.dt.uint16

P = 128
TOKENS = 512
EXPERTS = 8
PIECE = 128
ENTRIES = EXPERTS * PIECE
PIECE_COLS = PIECE // 16
SHARE = 2
SHARES = EXPERTS // SHARE
WIDTH = SHARE * PIECE
BLOCK = 8
BANK = 512
WARMUPS = 4

FLOPS = 2 * P * P * ENTRIES


def tile_gather_matmul_kernel(tc, table, w, c, offs, out):
    nc = tc.nc
    with (
        tc.tile_pool(name="held", bufs=1) as held,
        tc.psum_pool(name="psum", bufs=1) as psum,
    ):
        gain_columns = held.tile([P, SHARES, BLOCK], F32, name="gain_columns")
        nc.sync.dma_start(
            gain_columns[:, :, 0:SHARE], c.rearrange("o (t p s) -> p (o t) s", t=SHARES, s=SHARE)
        )

        offsets = held.tile([P, ENTRIES // 16], U16, name="offsets")
        nc.sync.dma_start(offsets[:], offs)

        tokens = held.tile([P, TOKENS], BF16, name="tokens")
        nc.sync.dma_start(tokens[:], table)

        weights = []
        for t in range(SHARES):
            matrices = held.tile([P, SHARE, P], BF16, name=f"weights{t}")
            nc.sync.dma_start(matrices[:], w[t * SHARE : (t + 1) * SHARE].rearrange("e k m -> k e m"))
            weights.append(matrices)

        primer = held.tile([P, 2], F32, name="primer")
        nc.gpsimd.memset(primer[:, 0:1], 0.0)
        nc.scalar.copy(primer[:, 1:2], primer[:, 0:1])

        identity = held.tile([P, P], F32, name="identity")
        make_identity(nc, identity[:])

        zero = held.tile([P, 1], BF16, name="zero")
        nc.vector.memset(zero[:], 0.0)
        unread = psum.tile([P, BANK], F32, name="unread")
        nc.tensor.matmul(
            unread[:], zero[:].to_broadcast([P, P]), zero[:].to_broadcast([P, BANK]), start=True, stop=True
        )
        for n in range(WARMUPS - 1):
            warm = psum.tile([P, BANK], F32, name=f"warm{n}", tag=f"own{n}")
            nc.tensor.matmul(
                warm[:], identity[:].bitcast(BF16)[:, 0:P], zero[:].to_broadcast([P, BANK]), start=True, stop=True
            )

        gains = held.tile([P, ENTRIES], F32, name="gains")
        for t in range(SHARES):
            spread = psum.tile([P, WIDTH], F32, name=f"spread{t}", tag=f"share{t}")
            for s in range(SHARE):
                nc.tensor.transpose(
                    spread[:, s * P : (s + 1) * P],
                    gain_columns[:, t, s : s + 1].to_broadcast([P, P]),
                    identity[:],
                )
            in_order = gains[:, t * WIDTH : (t + 1) * WIDTH].rearrange("m (p s) -> m p s", s=SHARE)
            as_spread = spread[:].rearrange("m (s p) -> m p s", s=SHARE)
            if t < SHARES // 2:
                nc.vector.tensor_copy(in_order, as_spread)
            else:
                nc.scalar.copy(in_order, as_spread)

        scaled = held.tile([P, ENTRIES], F32, name="scaled")

        pieces = [(e, 1) for e in range(SHARE)]
        pieces += [(t * SHARE, SHARE) for t in range(1, SHARES - 1)]
        pieces += [(e, 1) for e in range(EXPERTS - SHARE, EXPERTS)]
        slots = [f"own{n}" for n in range(WARMUPS - 1)] + [f"share{t}" for t in range(SHARES)]
        for n, (first, count) in enumerate(pieces):
            products = psum.tile([P, count * PIECE], F32, name=f"products{n}", tag=slots[n])
            for i in range(count):
                e = first + i
                picked = tokens[:].indirect(offsets[:, e * PIECE_COLS : (e + 1) * PIECE_COLS])
                nc.tensor.matmul(
                    products[:, i * PIECE : (i + 1) * PIECE],
                    weights[e // SHARE][:, e % SHARE, :],
                    picked,
                    start=True,
                    stop=True,
                )
            cols = slice(first * PIECE, (first + count) * PIECE)
            nc.vector.tensor_tensor(scaled[:, cols], products[:], gains[:, cols], mybir.AluOpType.mult)
            queue = nc.sync if n % 2 == 0 else nc.scalar
            queue.dma_start(out[:, cols], scaled[:, cols])
